import numpy as np, ml_dtypes
CORES = [9,41,49,65,73,81,97,113,15,47,55,71,79,87,103,119]
N = 16
import mx_ref
NC, ROOT = 128, 6
C = np.float32(0.047)
BF = ml_dtypes.bfloat16
def cut(t, i, w=512):
    return t[:, w * i:w * i + w]
def tile(rs):
    return np.stack(rs, axis=2).reshape(128, -1).astype(BF)
def pick(b):
    s = np.zeros((128, 128, 4), np.float32)
    s[np.arange(128), np.arange(128), b] = 1.0
    return mx_ref.quantize(s.reshape(128, 512).astype(BF))
def pk(c, s, i=0):
    return (np.ascontiguousarray(c[:, 512 * i:512 * i + 512]), mx_ref.live(s[:, 128 * i:128 * i + 128]))
def inputs(rng, e, E):
    def f(*shape):
        v = (rng.standard_normal(shape, dtype=np.float32) * np.exp2(rng.integers(-2, 3, shape[:-1] + (1,)))).astype(BF)
        return mx_ref.spread((v.astype(np.float32) * np.exp2(rng.integers(-E, E + 1, shape[:-2] + (1, 1))).astype(np.float32)).astype(BF), rng, e)
    def packed(k):
        c = np.zeros((N, 128, k * 512), np.uint8); s = np.zeros((N, 128, k * 128), np.uint8)
        for r in range(N):
            for i in range(k):
                a, b = mx_ref.quantize(f(128, 512)); c[r][:, 512 * i:512 * i + 512] = a; s[r][:, 128 * i:128 * i + 128] = mx_ref.plane(b, rng)
        return c, s
    d = {}
    d["wc"], d["ws"] = packed(1)
    d["a"] = f(N, 128, 512)
    d["bb"] = f(N, 128, 4 * 512)
    d["x"] = f(N, 128, 4 * NC)
    return d
def setup_inputs(rng):
    return inputs(rng, 0, 0)
def setup_inputs_blocks(rng):
    return inputs(rng, 2, 0)
def setup_inputs_wide(rng):
    return inputs(rng, 0, 3)
def reference(wc, ws, a, bb, x):
    S = [pick(t) for t in range(4)]; A = mx_ref.quantize(a[ROOT])
    V = [mx_ref.quantize(tile([mx_ref.matmul(S[t], pk(wc[j], ws[j])) + mx_ref.matmul(mx_ref.quantize(cut(bb[j], t)), A) * C for t in range(4)])) for j in range(N)]
    y = np.zeros((N, 128, N * NC), np.float32)
    for r in range(N):
        X = mx_ref.quantize(x[r])
        for j in range(N):
            y[r][:, NC * j:NC * j + NC] = mx_ref.matmul(V[j], X)
    return {"y": y}

@@ -1,0 +1,284 @@
+from concourse.bass import DstId, RemoteDMATransfer
+from concourse.mybir import dt, AluOpType, ActivationFunctionType
+
+NC = 128
+W4 = 4 * NC
+C = 0.047
+NR = 16
+
+SCRATCH = {
+    "ta": ("sbuf", [128, W4], "bfloat16"),
+    "tx": ("sbuf", [128, W4], "bfloat16"),
+    "tb": ("sbuf", [128, 4 * W4], "bfloat16"),
+    "ones": ("sbuf", [128, W4 + 8], "bfloat16"),
+    "sel": ("sbuf", [128, W4 + 8], "bfloat16"),
+    "tv": ("sbuf", [128, W4], "bfloat16"),
+    "tmp": ("sbuf", [128, W4], "float32"),
+    "yo": ("sbuf", [128, NR * NC], "float32"),
+    "aq": ("sbuf", [128, NC], "float8_e4m3fn_x4"),
+    "ap_": ("sbuf", [128, NC], "uint8"),
+    "xq": ("sbuf", [128, NC], "float8_e4m3fn_x4"),
+    "xp": ("sbuf", [128, NC], "uint8"),
+    "bq": ("sbuf", [128, 4 * NC], "float8_e4m3fn_x4"),
+    "bp": ("sbuf", [128, 4 * NC], "uint8"),
+    "sq": ("sbuf", [128, 4 * NC], "float8_e4m3fn_x4"),
+    "sp": ("sbuf", [128, 4 * NC], "uint8"),
+    "wq": ("sbuf", [128, NC], "float8_e4m3fn_x4"),
+    "wp": ("sbuf", [128, NC], "uint8"),
+    "vq": ("sbuf", [128, NR * NC], "float8_e4m3fn_x4"),
+    "vp": ("sbuf", [128, NR * NC], "uint8"),
+    "ps": ("psum", [128, 8 * 512], "float32"),
+}
+SEMAPHORES = (["ld_a", "ld_x", "ld_w", "ld_b", "st", "sent", "a1", "a2", "f0", "f1", "pe", "act", "dve", "gp"]
+              + ["t%d" % j for j in range(NR)])
+
+
+def make_plan(T, topo):
+    cores = list(T.cores)
+    n = len(cores)
+    chip = [topo.chip(c) for c in cores]
+    die = [topo.die(c) for c in cores]
+    root = T.root
+    every = range(topo.CHIPS * topo.CORES_PER_CHIP)
+
+    def near(p, q):
+        return p == q or topo.same_plane(p, q)
+
+    group = [0 if near(chip[r], chip[root]) else 1 for r in range(n)]
+    lanes = [die[root]] + [d for d in sorted(set(die)) if d != die[root]]
+    lane = [lanes.index(d) for d in die]
+    partner = [[q for q in range(n) if chip[q] == chip[r] and q != r][0] for r in range(n)]
+    members = {(l, k): [r for r in range(n) if lane[r] == l and group[r] == k] for l in (0, 1) for k in (0, 1)}
+    slot, base = {}, 0
+    span = {}
+    for l in (0, 1):
+        for k in (0, 1):
+            m = members[(l, k)]
+            span[(l, k)] = (base, base + len(m))
+            for r in m:
+                slot[r] = base
+                base += 1
+
+    def owners(r, d):
+        return [c for c in every if topo.chip(c) == chip[r] and topo.die(c) == die[r] and topo.may_write(c, d)]
+
+    near_dst, send = {}, {}
+    for r in range(n):
+        near_dst[r] = [q for q in members[(lane[r], group[r])] if q != r]
+        far = members[(lane[r], 1 - group[r])]
+        own = owners(r, cores[far[0]])
+        if cores[r] in own:
+            own = [c for c in own if c != cores[r]][:1] + [cores[r]]
+        own = own[:2]
+        cut = (len(far) + 1) // 2
+        send[r] = {own[0]: far[:cut], own[1]: far[cut:]}
+    far_chips = sorted(set(chip[r] for r in range(n) if group[r] == 1))
+    probe = cores[[r for r in range(n) if group[r] == 1][0]]
+    rel = [c for c in owners(root, probe) if c != cores[root]]
+    if topo.may_write(cores[partner[root]], probe):
+        rel = rel + [cores[partner[root]]]
+    a_relay = {}
+    for i, ch in enumerate(far_chips):
+        a_relay.setdefault(rel[i % len(rel)], []).extend([r for r in range(n) if chip[r] == ch])
+    return dict(cores=cores, n=n, chip=chip, group=group, lane=lane, partner=partner, members=members, slot=slot,
+                span=span, near_dst=near_dst, send=send, root=root, a_relay=a_relay)
+
+
+def rank_program(g, core, T, topo):
+    P = make_plan(T, topo)
+    cores, slot, root = P["cores"], P["slot"], P["root"]
+    rank = T.rank_of(core)
+    sem = T.sem
+    every = range(topo.CHIPS * topo.CORES_PER_CHIP)
+    MON = topo.mask(core, [c for c in every if c != core and topo.chip(c) == topo.chip(core)][0])
+    MOFF = topo.mask(core, [c for c in every if topo.same_plane(topo.chip(c), topo.chip(core))][0])
+    MUP = MON & ~MOFF
+    ne = {m: bin(m).count("1") for m in (MON, MOFF, MUP)}
+    sent = [0]
+
+    def codes(buf, lo, hi):
+        return T[buf][:, lo * NC:hi * NC].bitcast(dt.uint8)
+
+    def planes(buf, lo, hi):
+        return T[buf][:, lo * NC:hi * NC]
+
+    def call(parts, src, s):
+        tr = []
+        for m, dst in parts:
+            if not dst:
+                continue
+            ids = []
+            for d in dst:
+                rid, pid, _ = topo.addr(d)
+                ids.append(DstId(rid=rid, pnc=pid))
+            tr.append(RemoteDMATransfer(dst_ids=ids, dma_engine_mask=m, remote_sem=s, srcs=[src], dsts=[src] * len(ids)))
+            sent[0] += ne[m]
+        g.remote_dma_fused(tr, local_sem=sem.sent)
+
+    def send_tiles(parts, lo, hi, s):
+        call(parts, codes("vq", lo, hi), s)
+        call(parts, planes("vp", lo, hi), s)
+
+    def relay_a():
+        if core in P["a_relay"]:
+            dst = [cores[q] for q in P["a_relay"][core]]
+            call([(MOFF, dst)], codes("aq", 0, 1), sem.a1)
+            call([(MOFF, dst)], planes("ap_", 0, 1), sem.a1)
+
+    def relay_v(r):
+        dst = [cores[q] for q in P["send"][r].get(core, [])]
+        if dst:
+            send_tiles([(MOFF, dst)], slot[r], slot[r] + 1, sem["t%d" % r])
+
+    if rank is None:
+        if core in P["a_relay"]:
+            g.wait_ge(sem.a1, 2 * ne[MUP])
+            relay_a()
+        for r in range(P["n"]):
+            if core in P["send"][r]:
+                g.wait_ge(sem["t%d" % r], 2 * ne[MUP])
+                relay_v(r)
+        if sent[0]:
+            g.wait_ge(sem.sent, sent[0])
+        return
+
+    me = rank
+    lane, group, chip = P["lane"], P["group"], P["chip"]
+    mate = P["partner"][me]
+    cmate = cores[mate]
+    cnt = {"pe": 0, "act": 0, "dve": 0, "gp": 0}
+
+    def done(q, ins):
+        ins.then_inc(sem[q], 1)
+        cnt[q] += 1
+        return cnt[q]
+
+    if me == root:
+        g.sync.dma_start(T.ta[:], T.a[:]).then_inc(sem.ld_a, 16)
+    g.sync.dma_start(T.wq[:].bitcast(dt.uint8), T.wc[:]).then_inc(sem.ld_w, 16)
+    g.sync.dma_start(T.wp[:], T.ws[:]).then_inc(sem.ld_w, 16)
+    g.sync.dma_start(T.tx[:], T.x[:]).then_inc(sem.ld_x, 16)
+    g.sync.dma_start(T.tb[:], T.bb[:]).then_inc(sem.ld_b, 16)
+
+    i_ones = done("dve", g.vector.memset(T.ones[:], 1.0))
+    g.wait_ge(sem.dve, i_ones)
+    i_sel = done("gp", g.affine_select(T.sel[:], T.ones[:], [[-1, W4 + 8]], AluOpType.is_equal, 0.0, 3, 4))
+    if me == root:
+        g.vector.wait_ge(sem.ld_a, 16)
+        i_a = done("dve", g.vector.quantize_mx(T.aq[:], T.ap_[:], T.ta[:]))
+    g.vector.wait_ge(sem.gp, i_sel)
+    for b in range(4):
+        i_s = done("dve", g.vector.quantize_mx(T.sq[:, b * NC:(b + 1) * NC], T.sp[:, b * NC:(b + 1) * NC],
+                                               T.sel[:, 3 - b:3 - b + W4]))
+    g.vector.wait_ge(sem.ld_x, 16)
+    done("dve", g.vector.quantize_mx(T.xq[:], T.xp[:], T.tx[:]))
+    g.vector.wait_ge(sem.ld_b, 16)
+    i_b = done("dve", g.vector.quantize_mx(T.bq[:], T.bp[:], T.tb[:]))
+
+    a1 = a2 = 0
+    if me == root:
+        g.wait_ge(sem.dve, i_a)
+        here = [c for c in P["a_relay"] if c != cmate]
+        here = here + [cmate]
+        ev = sorted(set(chip[r] for r in range(P["n"]) if group[r] == group[me] and chip[r] != chip[me]))
+        l0 = [cores[r] for ch in ev for r in range(P["n"]) if chip[r] == ch and lane[r] == lane[me]]
+        l1 = [cores[r] for ch in ev for r in range(P["n"]) if chip[r] == ch and lane[r] != lane[me]]
+        call([(MUP, here), (MOFF, l0)], codes("aq", 0, 1), sem.a1)
+        call([(MUP, here), (MOFF, l1)], planes("ap_", 0, 1), sem.a1)
+    elif chip[me] == chip[root]:
+        a1 = 2 * ne[MUP]
+        g.wait_ge(sem.a1, a1)
+        relay_a()
+    elif group[me] != group[root]:
+        a1 = 2 * ne[MOFF]
+    else:
+        a1 = ne[MOFF]
+        a2 = ne[MON]
+        g.wait_ge(sem.a1, a1)
+        what = codes("aq", 0, 1) if lane[me] == lane[root] else planes("ap_", 0, 1)
+        call([(MON, [cmate])], what, sem.a2)
+
+    def bank(k):
+        return T.ps[:, 512 * k:512 * k + NC]
+
+    g.tensor.wait_ge(sem.dve, i_s)
+    g.tensor.wait_ge(sem.ld_w, 32)
+    for b in range(4):
+        i_d = done("pe", g.tensor.matmul_mx(bank(b), T.sq[:, b * NC:(b + 1) * NC], T.sp[:, b * NC:(b + 1) * NC],
+                                            T.wq[:], T.wp[:], True, True))
+    g.tensor.wait_ge(sem.dve, i_b)
+    if a1:
+        g.tensor.wait_ge(sem.a1, a1)
+    if a2:
+        g.tensor.wait_ge(sem.a2, a2)
+    for b in range(4):
+        i_m = done("pe", g.tensor.matmul_mx(bank(4 + b), T.bq[:, b * NC:(b + 1) * NC], T.bp[:, b * NC:(b + 1) * NC],
+                                            T.aq[:], T.ap_[:], True, True))
+        g.scalar.wait_ge(sem.pe, i_m)
+        i_c = done("act", g.scalar.activation(T.tmp[:, b * NC:(b + 1) * NC], bank(4 + b), ActivationFunctionType.Copy,
+                                              scale=C))
+        g.vector.wait_ge(sem.act, i_c)
+        i_v = done("dve", g.vector.tensor_tensor(T.tv[:, b:W4:4], bank(b), T.tmp[:, b * NC:(b + 1) * NC], AluOpType.add))
+    s0 = slot[me]
+    g.vector.wait_ge(sem.dve, i_v)
+    i_q = done("dve", g.vector.quantize_mx(T.vq[:, s0 * NC:(s0 + 1) * NC], T.vp[:, s0 * NC:(s0 + 1) * NC], T.tv[:]))
+
+    g.wait_ge(sem.dve, i_q)
+    mine = [cores[q] for q in P["send"][me].get(core, [])]
+    helpers = [c for c in P["send"][me] if c != core]
+    send_tiles([(MUP, helpers), (MOFF, mine + [cores[q] for q in P["near_dst"][me]])], s0, s0 + 1, sem["t%d" % me])
+    arr = 2 * ne[MOFF]
+    for k in (0, 1):
+        for r in P["members"][(lane[me], k)]:
+            if r != me:
+                g.wait_ge(sem["t%d" % r], arr)
+        lo, hi = P["span"][(lane[me], k)]
+        send_tiles([(MON, [cmate])], lo, hi, sem["f%d" % k])
+    g.wait_ge(sem.sent, sent[0])
+
+    order = [(me, None)]
+    for k in (0, 1):
+        order += [(r, "t%d" % r) for r in P["members"][(lane[me], k)] if r != me]
+        order += [(r, "f%d" % k) for r in P["members"][(1 - lane[me], k)]]
+    copied = []
+    where = {}
+    g.tensor.wait_ge(sem.dve, i_q)
+    seen = set()
+    for i, (r, s) in enumerate(order):
+        if s is not None and s not in seen:
+            seen.add(s)
+            g.tensor.wait_ge(sem[s], arr if s[0] == "t" else 2 * ne[MON])
+        if i >= 8:
+            g.tensor.wait_ge(sem[copied[i - 8][0]], copied[i - 8][1])
+        sl = slot[r]
+        i_y = done("pe", g.tensor.matmul_mx(bank(i % 8), T.vq[:, sl * NC:(sl + 1) * NC], T.vp[:, sl * NC:(sl + 1) * NC],
+                                            T.xq[:], T.xp[:], True, True))
+        dst = T.yo[:, r * NC:(r + 1) * NC]
+        if i % 2 == 0:
+            g.vector.wait_ge(sem.pe, i_y)
+            c = ("dve", done("dve", g.vector.tensor_copy(dst, bank(i % 8))))
+        else:
+            g.scalar.wait_ge(sem.pe, i_y)
+            c = ("act", done("act", g.scalar.activation(dst, bank(i % 8), ActivationFunctionType.Copy)))
+        copied.append(c)
+        where[r] = c
+    nst = 0
+    for k in (0, 1):
+        for l in (lane[me], 1 - lane[me]):
+            m = sorted(P["members"][(l, k)])
+            runs = []
+            for r in m:
+                if runs and runs[-1][-1] == r - 1:
+                    runs[-1].append(r)
+                else:
+                    runs.append([r])
+            for run in runs:
+                need = {}
+                for r in run:
+                    q, v = where[r]
+                    need[q] = max(need.get(q, 0), v)
+                for q in sorted(need):
+                    g.sync.wait_ge(sem[q], need[q])
+                g.sync.dma_start(T.y[:, run[0] * NC:(run[-1] + 1) * NC], T.yo[:, run[0] * NC:(run[-1] + 1) * NC]).then_inc(sem.st, 16)
+                nst += 16
+    g.sync.wait_ge(sem.st, nst)

@@ -5,13 +5,18 @@ NC = 128
 W4 = 4 * NC
 C = 0.047
 NR = 16
+SPLIT = {
+    0: {5: [("self", 4, 0), ("o1", 0, 2), ("o2", 0, 1)], 3: [("self", 2, 0), ("o1", 0, 3), ("o2", 0, 2)]},
+    1: {5: [("self", 4, 1), ("o1", 0, 2)], 3: [("self", 0, 4), ("o1", 2, 1)]},
+}
 
 SCRATCH = {
     "ta": ("sbuf", [128, W4], "bfloat16"),
     "tx": ("sbuf", [128, W4], "bfloat16"),
     "tb": ("sbuf", [128, 4 * W4], "bfloat16"),
-    "ones": ("sbuf", [128, W4 + 8], "bfloat16"),
-    "sel": ("sbuf", [128, W4 + 8], "bfloat16"),
+    "ones": ("sbuf", [128, NC], "bfloat16"),
+    "eye": ("sbuf", [128, NC], "bfloat16"),
+    "sel": ("sbuf", [128, W4], "bfloat16"),
     "tv": ("sbuf", [128, W4], "bfloat16"),
     "tmp": ("sbuf", [128, W4], "float32"),
     "yo": ("sbuf", [128, NR * NC], "float32"),
@@ -29,8 +34,8 @@ SCRATCH = {
     "vp": ("sbuf", [128, NR * NC], "uint8"),
     "ps": ("psum", [128, 8 * 512], "float32"),
 }
-SEMAPHORES = (["ld_a", "ld_x", "ld_w", "ld_b", "st", "sent", "a1", "a2", "f0", "f1", "pe", "act", "dve", "gp"]
-              + ["t%d" % j for j in range(NR)])
+SEMAPHORES = (["ld_a", "ld_x", "ld_w", "ld_b", "st", "sent", "s_in", "a2", "pe", "act", "dve", "gp"]
+              + [k + x for k in ["a1", "f0", "f1"] + ["t%d" % j for j in range(NR)] for x in "cp"])
 
 
 def make_plan(T, topo):
@@ -47,60 +52,76 @@ def make_plan(T, topo):
     group = [0 if near(chip[r], chip[root]) else 1 for r in range(n)]
     lanes = [die[root]] + [d for d in sorted(set(die)) if d != die[root]]
     lane = [lanes.index(d) for d in die]
-    partner = [[q for q in range(n) if chip[q] == chip[r] and q != r][0] for r in range(n)]
-    members = {(l, k): [r for r in range(n) if lane[r] == l and group[r] == k] for l in (0, 1) for k in (0, 1)}
-    slot, base = {}, 0
-    span = {}
+    at = {(chip[r], lane[r]): r for r in range(n)}
+    partner = [at[(chip[r], 1 - lane[r])] for r in range(n)]
+    gchips = [[chip[r] for r in range(n) if group[r] == k and lane[r] == 0] for k in (0, 1)]
+    members, span, slot = {}, {}, {}
     for l in (0, 1):
         for k in (0, 1):
-            m = members[(l, k)]
-            span[(l, k)] = (base, base + len(m))
+            m = [at[(ch, l)] for ch in gchips[k]]
+            members[(l, k)] = m
+            span[(l, k)] = (len(slot) * NC, (len(slot) + len(m)) * NC)
             for r in m:
-                slot[r] = base
-                base += 1
-
-    def owners(r, d):
-        return [c for c in every if topo.chip(c) == chip[r] and topo.die(c) == die[r] and topo.may_write(c, d)]
-
-    near_dst, send = {}, {}
+                slot[r] = len(slot)
+    send, helpers = {}, {}
     for r in range(n):
-        near_dst[r] = [q for q in members[(lane[r], group[r])] if q != r]
-        far = members[(lane[r], 1 - group[r])]
-        own = owners(r, cores[far[0]])
-        if cores[r] in own:
-            own = [c for c in own if c != cores[r]][:1] + [cores[r]]
-        own = own[:2]
-        cut = (len(far) + 1) // 2
-        send[r] = {own[0]: far[:cut], own[1]: far[cut:]}
-    far_chips = sorted(set(chip[r] for r in range(n) if group[r] == 1))
-    probe = cores[[r for r in range(n) if group[r] == 1][0]]
-    rel = [c for c in owners(root, probe) if c != cores[root]]
-    if topo.may_write(cores[partner[root]], probe):
-        rel = rel + [cores[partner[root]]]
+        g0, g1 = gchips[group[r]], gchips[1 - group[r]]
+        i = g0.index(chip[r])
+        nr = g0[i + 1:] + g0[:i]
+        k = (i * len(g1)) // len(g0)
+        fr = g1[k:] + g1[:k]
+        other = cores[at[(fr[0], 0)]]
+        own = [c for c in every if topo.chip(c) == chip[r] and topo.die(c) == die[r] and c != cores[r]
+               and topo.may_write(c, other)]
+        who = {"self": cores[r]}
+        for j, c in enumerate(own):
+            who["o%d" % (j + 1)] = c
+        send[r] = {}
+        for w, a, b in SPLIT[lane[r]][len(g0)]:
+            send[r][who[w]] = [at[(ch, lane[r])] for ch in fr[:b] + nr[:a]]
+            nr, fr = nr[a:], fr[b:]
+        helpers[r] = [c for c in send[r] if c != cores[r]]
+    s_part, s_calls = {}, {}
+    for ch in sorted(set(chip)):
+        two = [at[(ch, 0)], at[(ch, 1)]]
+        both = [cores[r] for r in two]
+        h = helpers[two[0]] + helpers[two[1]]
+        half = len(h) // 2
+        for t, hs in ((0, h[:half]), (1, h[half:])):
+            w = NC // len(hs)
+            for i, c in enumerate(hs):
+                s_part[c] = (t, i * w, (i + 1) * w, both)
+        for i in (0, 1):
+            s_part[both[i]] = (2 + i, 0, NC, [both[1 - i]])
+            s_calls[two[i]] = 2 * (len(h) + 1)
+    other = cores[at[(gchips[1][0], 0)]]
+    rel = [c for r in (root, partner[root]) for c in [cores[r]] + helpers[r] if c != cores[root] and topo.may_write(c, other)]
     a_relay = {}
-    for i, ch in enumerate(far_chips):
-        a_relay.setdefault(rel[i % len(rel)], []).extend([r for r in range(n) if chip[r] == ch])
-    return dict(cores=cores, n=n, chip=chip, group=group, lane=lane, partner=partner, members=members, slot=slot,
-                span=span, near_dst=near_dst, send=send, root=root, a_relay=a_relay)
+    for i, ch in enumerate(gchips[1]):
+        a_relay.setdefault(rel[i % len(rel)], []).extend([cores[at[(ch, 0)]], cores[at[(ch, 1)]]])
+    return dict(cores=cores, n=n, chip=chip, group=group, lane=lane, partner=partner, at=at, gchips=gchips, root=root,
+                members=members, span=span, slot=slot, send=send, helpers=helpers, a_relay=a_relay, s_part=s_part,
+                s_calls=s_calls)
 
 
 def rank_program(g, core, T, topo):
     P = make_plan(T, topo)
-    cores, slot, root = P["cores"], P["slot"], P["root"]
+    cores, root, slot, lane, at = P["cores"], P["root"], P["slot"], P["lane"], P["at"]
     rank = T.rank_of(core)
     sem = T.sem
+    here = topo.chip(core)
     every = range(topo.CHIPS * topo.CORES_PER_CHIP)
-    MON = topo.mask(core, [c for c in every if c != core and topo.chip(c) == topo.chip(core)][0])
-    MOFF = topo.mask(core, [c for c in every if topo.same_plane(topo.chip(c), topo.chip(core))][0])
+    MON = topo.mask(core, [c for c in every if c != core and topo.chip(c) == here][0])
+    MOFF = topo.mask(core, [c for c in every if topo.same_plane(topo.chip(c), here)][0])
     MUP = MON & ~MOFF
     ne = {m: bin(m).count("1") for m in (MON, MOFF, MUP)}
     sent = [0]
+    cnt = {"pe": 0, "act": 0, "dve": 0, "gp": 0}
 
-    def codes(buf, lo, hi):
-        return T[buf][:, lo * NC:hi * NC].bitcast(dt.uint8)
-
-    def planes(buf, lo, hi):
-        return T[buf][:, lo * NC:hi * NC]
+    def done(q, ins):
+        ins.then_inc(sem[q], 1)
+        cnt[q] += 1
+        return cnt[q]
 
     def call(parts, src, s):
         tr = []
@@ -115,43 +136,59 @@ def rank_program(g, core, T, topo):
             sent[0] += ne[m]
         g.remote_dma_fused(tr, local_sem=sem.sent)
 
-    def send_tiles(parts, lo, hi, s):
-        call(parts, codes("vq", lo, hi), s)
-        call(parts, planes("vp", lo, hi), s)
+    def send_c(parts, buf, lo, hi, s):
+        call(parts, T[buf][:, lo:hi].bitcast(dt.uint8), sem[s])
+
+    def send_p(parts, buf, lo, hi, s):
+        call(parts, T[buf][:, lo:hi], sem[s])
+
+    def send_v(parts, lo, hi, s, need=(), count=0):
+        for q in need:
+            g.wait_ge(sem[q + "c"], count)
+        send_c(parts, "vq", lo, hi, s + "c")
+        for q in need:
+            g.wait_ge(sem[q + "p"], count)
+        send_p(parts, "vp", lo, hi, s + "p")
+
+    def selector(tile, lo, hi, dst):
+        i_ones = done("dve", g.vector.memset(T.ones[:], 1.0))
+        g.wait_ge(sem.dve, i_ones)
+        i_eye = done("gp", g.affine_select(T.eye[:], T.ones[:], [[-1, NC]], AluOpType.is_equal, 0.0, 0, 1))
+        i_z = done("dve", g.vector.memset(T.sel[:], 0.0))
+        g.vector.wait_ge(sem.gp, i_eye)
+        g.vector.wait_ge(sem.dve, i_z)
+        i_t = done("dve", g.vector.tensor_copy(T.sel[:, tile:W4:4], T.eye[:]))
+        g.vector.wait_ge(sem.dve, i_t)
+        o = tile * NC
+        i_q = done("dve", g.vector.quantize_mx(T.sq[:, o:o + NC], T.sp[:, o:o + NC], T.sel[:]))
+        g.wait_ge(sem.dve, i_q)
+        send_c([(MON, dst)], "sq", o + lo, o + hi, "s_in")
+        send_p([(MON, dst)], "sp", o + lo, o + hi, "s_in")
+        return i_q
 
     def relay_a():
-        if core in P["a_relay"]:
-            dst = [cores[q] for q in P["a_relay"][core]]
-            call([(MOFF, dst)], codes("aq", 0, 1), sem.a1)
-            call([(MOFF, dst)], planes("ap_", 0, 1), sem.a1)
-
-    def relay_v(r):
-        dst = [cores[q] for q in P["send"][r].get(core, [])]
+        dst = P["a_relay"].get(core)
         if dst:
-            send_tiles([(MOFF, dst)], slot[r], slot[r] + 1, sem["t%d" % r])
+            g.wait_ge(sem.a1c, ne[MUP])
+            send_c([(MOFF, dst)], "aq", 0, NC, "a1c")
+            g.wait_ge(sem.a1p, ne[MUP])
+            send_p([(MOFF, dst)], "ap_", 0, NC, "a1p")
 
     if rank is None:
-        if core in P["a_relay"]:
-            g.wait_ge(sem.a1, 2 * ne[MUP])
-            relay_a()
+        if core in P["s_part"]:
+            selector(*P["s_part"][core])
+        relay_a()
         for r in range(P["n"]):
-            if core in P["send"][r]:
-                g.wait_ge(sem["t%d" % r], 2 * ne[MUP])
-                relay_v(r)
+            if core in P["helpers"][r]:
+                lo = slot[r] * NC
+                send_v([(MOFF, [cores[q] for q in P["send"][r][core]])], lo, lo + NC, "t%d" % r, ["t%d" % r], ne[MUP])
         if sent[0]:
             g.wait_ge(sem.sent, sent[0])
         return
 
     me = rank
-    lane, group, chip = P["lane"], P["group"], P["chip"]
-    mate = P["partner"][me]
-    cmate = cores[mate]
-    cnt = {"pe": 0, "act": 0, "dve": 0, "gp": 0}
-
-    def done(q, ins):
-        ins.then_inc(sem[q], 1)
-        cnt[q] += 1
-        return cnt[q]
+    group, chip = P["group"], P["chip"]
+    cmate = cores[P["partner"][me]]
 
     if me == root:
         g.sync.dma_start(T.ta[:], T.a[:]).then_inc(sem.ld_a, 16)
@@ -160,99 +197,91 @@ def rank_program(g, core, T, topo):
     g.sync.dma_start(T.tx[:], T.x[:]).then_inc(sem.ld_x, 16)
     g.sync.dma_start(T.tb[:], T.bb[:]).then_inc(sem.ld_b, 16)
 
-    i_ones = done("dve", g.vector.memset(T.ones[:], 1.0))
-    g.wait_ge(sem.dve, i_ones)
-    i_sel = done("gp", g.affine_select(T.sel[:], T.ones[:], [[-1, W4 + 8]], AluOpType.is_equal, 0.0, 3, 4))
+    i_s = selector(*P["s_part"][core])
     if me == root:
         g.vector.wait_ge(sem.ld_a, 16)
         i_a = done("dve", g.vector.quantize_mx(T.aq[:], T.ap_[:], T.ta[:]))
-    g.vector.wait_ge(sem.gp, i_sel)
-    for b in range(4):
-        i_s = done("dve", g.vector.quantize_mx(T.sq[:, b * NC:(b + 1) * NC], T.sp[:, b * NC:(b + 1) * NC],
-                                               T.sel[:, 3 - b:3 - b + W4]))
     g.vector.wait_ge(sem.ld_x, 16)
     done("dve", g.vector.quantize_mx(T.xq[:], T.xp[:], T.tx[:]))
     g.vector.wait_ge(sem.ld_b, 16)
     i_b = done("dve", g.vector.quantize_mx(T.bq[:], T.bp[:], T.tb[:]))
 
-    a1 = a2 = 0
+    a_need = {}
     if me == root:
         g.wait_ge(sem.dve, i_a)
-        here = [c for c in P["a_relay"] if c != cmate]
-        here = here + [cmate]
-        ev = sorted(set(chip[r] for r in range(P["n"]) if group[r] == group[me] and chip[r] != chip[me]))
-        l0 = [cores[r] for ch in ev for r in range(P["n"]) if chip[r] == ch and lane[r] == lane[me]]
-        l1 = [cores[r] for ch in ev for r in range(P["n"]) if chip[r] == ch and lane[r] != lane[me]]
-        call([(MUP, here), (MOFF, l0)], codes("aq", 0, 1), sem.a1)
-        call([(MUP, here), (MOFF, l1)], planes("ap_", 0, 1), sem.a1)
-    elif chip[me] == chip[root]:
-        a1 = 2 * ne[MUP]
-        g.wait_ge(sem.a1, a1)
+        inside = [c for c in P["a_relay"] if c != cmate] + [cmate]
+        ev = [ch for ch in P["gchips"][0] if ch != here]
+        send_c([(MUP, inside), (MOFF, [cores[at[(ch, lane[me])]] for ch in ev])], "aq", 0, NC, "a1c")
+        send_p([(MUP, inside), (MOFF, [cores[at[(ch, 1 - lane[me])]] for ch in ev])], "ap_", 0, NC, "a1p")
+    elif here == chip[root]:
+        a_need = {"a1c": ne[MUP], "a1p": ne[MUP]}
         relay_a()
     elif group[me] != group[root]:
-        a1 = 2 * ne[MOFF]
+        a_need = {"a1c": ne[MOFF], "a1p": ne[MOFF]}
+    elif lane[me] == lane[root]:
+        a_need = {"a1c": ne[MOFF], "a2": ne[MON]}
+        g.wait_ge(sem.a1c, ne[MOFF])
+        send_c([(MON, [cmate])], "aq", 0, NC, "a2")
     else:
-        a1 = ne[MOFF]
-        a2 = ne[MON]
-        g.wait_ge(sem.a1, a1)
-        what = codes("aq", 0, 1) if lane[me] == lane[root] else planes("ap_", 0, 1)
-        call([(MON, [cmate])], what, sem.a2)
+        a_need = {"a1p": ne[MOFF], "a2": ne[MON]}
+        g.wait_ge(sem.a1p, ne[MOFF])
+        send_p([(MON, [cmate])], "ap_", 0, NC, "a2")
 
     def bank(k):
         return T.ps[:, 512 * k:512 * k + NC]
 
+    def tmp(b):
+        return T.tmp[:, b * NC:(b + 1) * NC]
+
     g.tensor.wait_ge(sem.dve, i_s)
+    g.tensor.wait_ge(sem.s_in, P["s_calls"][me] * ne[MON])
     g.tensor.wait_ge(sem.ld_w, 32)
     for b in range(4):
-        i_d = done("pe", g.tensor.matmul_mx(bank(b), T.sq[:, b * NC:(b + 1) * NC], T.sp[:, b * NC:(b + 1) * NC],
-                                            T.wq[:], T.wp[:], True, True))
+        done("pe", g.tensor.matmul_mx(bank(b), T.sq[:, b * NC:(b + 1) * NC], T.sp[:, b * NC:(b + 1) * NC],
+                                      T.wq[:], T.wp[:], True, True))
     g.tensor.wait_ge(sem.dve, i_b)
-    if a1:
-        g.tensor.wait_ge(sem.a1, a1)
-    if a2:
-        g.tensor.wait_ge(sem.a2, a2)
-    for b in range(4):
-        i_m = done("pe", g.tensor.matmul_mx(bank(4 + b), T.bq[:, b * NC:(b + 1) * NC], T.bp[:, b * NC:(b + 1) * NC],
-                                            T.aq[:], T.ap_[:], True, True))
-        g.scalar.wait_ge(sem.pe, i_m)
-        i_c = done("act", g.scalar.activation(T.tmp[:, b * NC:(b + 1) * NC], bank(4 + b), ActivationFunctionType.Copy,
-                                              scale=C))
-        g.vector.wait_ge(sem.act, i_c)
-        i_v = done("dve", g.vector.tensor_tensor(T.tv[:, b:W4:4], bank(b), T.tmp[:, b * NC:(b + 1) * NC], AluOpType.add))
-    s0 = slot[me]
+    for q in sorted(a_need):
+        g.tensor.wait_ge(sem[q], a_need[q])
+    i_m = [done("pe", g.tensor.matmul_mx(bank(4 + b), T.bq[:, b * NC:(b + 1) * NC], T.bp[:, b * NC:(b + 1) * NC],
+                                         T.aq[:], T.ap_[:], True, True)) for b in range(4)]
+    g.vector.wait_ge(sem.pe, i_m[0])
+    i_0 = done("dve", g.vector.tensor_scalar(tmp(0), bank(4), C, None, AluOpType.mult))
+    for b in (1, 0, 2, 3):
+        if b:
+            g.scalar.wait_ge(sem.pe, i_m[b])
+            i_c = done("act", g.scalar.activation(tmp(b), bank(4 + b), ActivationFunctionType.Copy, scale=C))
+            g.vector.wait_ge(sem.act, i_c)
+        else:
+            g.vector.wait_ge(sem.dve, i_0)
+        i_v = done("dve", g.vector.tensor_tensor(T.tv[:, b:W4:4], bank(b), tmp(b), AluOpType.add))
+    s0 = slot[me] * NC
     g.vector.wait_ge(sem.dve, i_v)
-    i_q = done("dve", g.vector.quantize_mx(T.vq[:, s0 * NC:(s0 + 1) * NC], T.vp[:, s0 * NC:(s0 + 1) * NC], T.tv[:]))
+    i_q = done("dve", g.vector.quantize_mx(T.vq[:, s0:s0 + NC], T.vp[:, s0:s0 + NC], T.tv[:]))
 
     g.wait_ge(sem.dve, i_q)
-    mine = [cores[q] for q in P["send"][me].get(core, [])]
-    helpers = [c for c in P["send"][me] if c != core]
-    send_tiles([(MUP, helpers), (MOFF, mine + [cores[q] for q in P["near_dst"][me]])], s0, s0 + 1, sem["t%d" % me])
-    arr = 2 * ne[MOFF]
+    send_v([(MUP, P["helpers"][me]), (MOFF, [cores[q] for q in P["send"][me][core]])], s0, s0 + NC, "t%d" % me)
     for k in (0, 1):
-        for r in P["members"][(lane[me], k)]:
-            if r != me:
-                g.wait_ge(sem["t%d" % r], arr)
         lo, hi = P["span"][(lane[me], k)]
-        send_tiles([(MON, [cmate])], lo, hi, sem["f%d" % k])
+        send_v([(MON, [cmate])], lo, hi, "f%d" % k,
+               ["t%d" % r for r in P["members"][(lane[me], k)] if r != me], ne[MOFF])
     g.wait_ge(sem.sent, sent[0])
 
     order = [(me, None)]
     for k in (0, 1):
         order += [(r, "t%d" % r) for r in P["members"][(lane[me], k)] if r != me]
         order += [(r, "f%d" % k) for r in P["members"][(1 - lane[me], k)]]
-    copied = []
-    where = {}
+    copied, where, seen = [], {}, set()
     g.tensor.wait_ge(sem.dve, i_q)
-    seen = set()
     for i, (r, s) in enumerate(order):
         if s is not None and s not in seen:
             seen.add(s)
-            g.tensor.wait_ge(sem[s], arr if s[0] == "t" else 2 * ne[MON])
+            for x in "cp":
+                g.tensor.wait_ge(sem[s + x], ne[MOFF] if s[0] == "t" else ne[MON])
         if i >= 8:
             g.tensor.wait_ge(sem[copied[i - 8][0]], copied[i - 8][1])
-        sl = slot[r]
-        i_y = done("pe", g.tensor.matmul_mx(bank(i % 8), T.vq[:, sl * NC:(sl + 1) * NC], T.vp[:, sl * NC:(sl + 1) * NC],
-                                            T.xq[:], T.xp[:], True, True))
+        lo = slot[r] * NC
+        i_y = done("pe", g.tensor.matmul_mx(bank(i % 8), T.vq[:, lo:lo + NC], T.vp[:, lo:lo + NC], T.xq[:], T.xp[:],
+                                            True, True))
         dst = T.yo[:, r * NC:(r + 1) * NC]
         if i % 2 == 0:
             g.vector.wait_ge(sem.pe, i_y)
@@ -265,9 +294,8 @@ def rank_program(g, core, T, topo):
     nst = 0
     for k in (0, 1):
         for l in (lane[me], 1 - lane[me]):
-            m = sorted(P["members"][(l, k)])
             runs = []
-            for r in m:
+            for r in sorted(P["members"][(l, k)]):
                 if runs and runs[-1][-1] == r - 1:
                     runs[-1].append(r)
                 else:
@@ -279,6 +307,7 @@ def rank_program(g, core, T, topo):
                     need[q] = max(need.get(q, 0), v)
                 for q in sorted(need):
                     g.sync.wait_ge(sem[q], need[q])
-                g.sync.dma_start(T.y[:, run[0] * NC:(run[-1] + 1) * NC], T.yo[:, run[0] * NC:(run[-1] + 1) * NC]).then_inc(sem.st, 16)
+                c0, c1 = run[0] * NC, (run[-1] + 1) * NC
+                g.sync.dma_start(T.y[:, c0:c1], T.yo[:, c0:c1]).then_inc(sem.st, 16)
                 nst += 16
     g.sync.wait_ge(sem.st, nst)

from concourse.bass import DstId, RemoteDMATransfer
from concourse.mybir import dt, AluOpType, ActivationFunctionType

NC = 128
W4 = 4 * NC
C = 0.047
NR = 16
SPLIT = {
    0: {5: [("self", 4, 0), ("o1", 0, 2), ("o2", 0, 1)], 3: [("self", 2, 0), ("o1", 0, 3), ("o2", 0, 2)]},
    1: {5: [("self", 4, 1), ("o1", 0, 2)], 3: [("self", 0, 4), ("o1", 2, 1)]},
}

SCRATCH = {
    "ta": ("sbuf", [128, W4], "bfloat16"),
    "tx": ("sbuf", [128, W4], "bfloat16"),
    "tb": ("sbuf", [128, 4 * W4], "bfloat16"),
    "ones": ("sbuf", [128, NC], "bfloat16"),
    "eye": ("sbuf", [128, NC], "bfloat16"),
    "sel": ("sbuf", [128, W4], "bfloat16"),
    "tv": ("sbuf", [128, W4], "bfloat16"),
    "tmp": ("sbuf", [128, W4], "float32"),
    "yo": ("sbuf", [128, NR * NC], "float32"),
    "aq": ("sbuf", [128, NC], "float8_e4m3fn_x4"),
    "ap_": ("sbuf", [128, NC], "uint8"),
    "xq": ("sbuf", [128, NC], "float8_e4m3fn_x4"),
    "xp": ("sbuf", [128, NC], "uint8"),
    "bq": ("sbuf", [128, 4 * NC], "float8_e4m3fn_x4"),
    "bp": ("sbuf", [128, 4 * NC], "uint8"),
    "sq": ("sbuf", [128, 4 * NC], "float8_e4m3fn_x4"),
    "sp": ("sbuf", [128, 4 * NC], "uint8"),
    "wq": ("sbuf", [128, NC], "float8_e4m3fn_x4"),
    "wp": ("sbuf", [128, NC], "uint8"),
    "vq": ("sbuf", [128, NR * NC], "float8_e4m3fn_x4"),
    "vp": ("sbuf", [128, NR * NC], "uint8"),
    "ps": ("psum", [128, 8 * 512], "float32"),
}
SEMAPHORES = (["ld_a", "ld_x", "ld_w", "ld_b", "st", "sent", "s_in", "a2", "pe", "act", "dve", "gp"]
              + [k + x for k in ["a1", "f0", "f1"] + ["t%d" % j for j in range(NR)] for x in "cp"])


def make_plan(T, topo):
    cores = list(T.cores)
    n = len(cores)
    chip = [topo.chip(c) for c in cores]
    die = [topo.die(c) for c in cores]
    root = T.root
    every = range(topo.CHIPS * topo.CORES_PER_CHIP)

    def near(p, q):
        return p == q or topo.same_plane(p, q)

    group = [0 if near(chip[r], chip[root]) else 1 for r in range(n)]
    lanes = [die[root]] + [d for d in sorted(set(die)) if d != die[root]]
    lane = [lanes.index(d) for d in die]
    at = {(chip[r], lane[r]): r for r in range(n)}
    partner = [at[(chip[r], 1 - lane[r])] for r in range(n)]
    gchips = [[chip[r] for r in range(n) if group[r] == k and lane[r] == 0] for k in (0, 1)]
    members, span, slot = {}, {}, {}
    for l in (0, 1):
        for k in (0, 1):
            m = [at[(ch, l)] for ch in gchips[k]]
            members[(l, k)] = m
            span[(l, k)] = (len(slot) * NC, (len(slot) + len(m)) * NC)
            for r in m:
                slot[r] = len(slot)
    send, helpers = {}, {}
    for r in range(n):
        g0, g1 = gchips[group[r]], gchips[1 - group[r]]
        i = g0.index(chip[r])
        nr = g0[i + 1:] + g0[:i]
        k = (i * len(g1)) // len(g0)
        fr = g1[k:] + g1[:k]
        other = cores[at[(fr[0], 0)]]
        own = [c for c in every if topo.chip(c) == chip[r] and topo.die(c) == die[r] and c != cores[r]
               and topo.may_write(c, other)]
        who = {"self": cores[r]}
        for j, c in enumerate(own):
            who["o%d" % (j + 1)] = c
        send[r] = {}
        for w, a, b in SPLIT[lane[r]][len(g0)]:
            send[r][who[w]] = [at[(ch, lane[r])] for ch in fr[:b] + nr[:a]]
            nr, fr = nr[a:], fr[b:]
        helpers[r] = [c for c in send[r] if c != cores[r]]
    s_part, s_calls = {}, {}
    for ch in sorted(set(chip)):
        two = [at[(ch, 0)], at[(ch, 1)]]
        both = [cores[r] for r in two]
        h = helpers[two[0]] + helpers[two[1]]
        half = len(h) // 2
        for t, hs in ((0, h[:half]), (1, h[half:])):
            w = NC // len(hs)
            for i, c in enumerate(hs):
                s_part[c] = (t, i * w, (i + 1) * w, both)
        for i in (0, 1):
            s_part[both[i]] = (2 + i, 0, NC, [both[1 - i]])
            s_calls[two[i]] = 2 * (len(h) + 1)
    other = cores[at[(gchips[1][0], 0)]]
    rel = [c for r in (root, partner[root]) for c in [cores[r]] + helpers[r] if c != cores[root] and topo.may_write(c, other)]
    a_relay = {}
    for i, ch in enumerate(gchips[1]):
        a_relay.setdefault(rel[i % len(rel)], []).extend([cores[at[(ch, 0)]], cores[at[(ch, 1)]]])
    return dict(cores=cores, n=n, chip=chip, group=group, lane=lane, partner=partner, at=at, gchips=gchips, root=root,
                members=members, span=span, slot=slot, send=send, helpers=helpers, a_relay=a_relay, s_part=s_part,
                s_calls=s_calls)


def rank_program(g, core, T, topo):
    P = make_plan(T, topo)
    cores, root, slot, lane, at = P["cores"], P["root"], P["slot"], P["lane"], P["at"]
    rank = T.rank_of(core)
    sem = T.sem
    here = topo.chip(core)
    every = range(topo.CHIPS * topo.CORES_PER_CHIP)
    MON = topo.mask(core, [c for c in every if c != core and topo.chip(c) == here][0])
    MOFF = topo.mask(core, [c for c in every if topo.same_plane(topo.chip(c), here)][0])
    MUP = MON & ~MOFF
    ne = {m: bin(m).count("1") for m in (MON, MOFF, MUP)}
    sent = [0]
    cnt = {"pe": 0, "act": 0, "dve": 0, "gp": 0}

    def done(q, ins):
        ins.then_inc(sem[q], 1)
        cnt[q] += 1
        return cnt[q]

    def call(parts, src, s):
        tr = []
        for m, dst in parts:
            if not dst:
                continue
            ids = []
            for d in dst:
                rid, pid, _ = topo.addr(d)
                ids.append(DstId(rid=rid, pnc=pid))
            tr.append(RemoteDMATransfer(dst_ids=ids, dma_engine_mask=m, remote_sem=s, srcs=[src], dsts=[src] * len(ids)))
            sent[0] += ne[m]
        g.remote_dma_fused(tr, local_sem=sem.sent)

    def send_c(parts, buf, lo, hi, s):
        call(parts, T[buf][:, lo:hi].bitcast(dt.uint8), sem[s])

    def send_p(parts, buf, lo, hi, s):
        call(parts, T[buf][:, lo:hi], sem[s])

    def send_v(parts, lo, hi, s, need=(), count=0):
        for q in need:
            g.wait_ge(sem[q + "c"], count)
        send_c(parts, "vq", lo, hi, s + "c")
        for q in need:
            g.wait_ge(sem[q + "p"], count)
        send_p(parts, "vp", lo, hi, s + "p")

    def selector(tile, lo, hi, dst):
        i_ones = done("dve", g.vector.memset(T.ones[:], 1.0))
        g.wait_ge(sem.dve, i_ones)
        i_eye = done("gp", g.affine_select(T.eye[:], T.ones[:], [[-1, NC]], AluOpType.is_equal, 0.0, 0, 1))
        i_z = done("dve", g.vector.memset(T.sel[:], 0.0))
        g.vector.wait_ge(sem.gp, i_eye)
        g.vector.wait_ge(sem.dve, i_z)
        i_t = done("dve", g.vector.tensor_copy(T.sel[:, tile:W4:4], T.eye[:]))
        g.vector.wait_ge(sem.dve, i_t)
        o = tile * NC
        i_q = done("dve", g.vector.quantize_mx(T.sq[:, o:o + NC], T.sp[:, o:o + NC], T.sel[:]))
        g.wait_ge(sem.dve, i_q)
        send_c([(MON, dst)], "sq", o + lo, o + hi, "s_in")
        send_p([(MON, dst)], "sp", o + lo, o + hi, "s_in")
        return i_q

    def relay_a():
        dst = P["a_relay"].get(core)
        if dst:
            g.wait_ge(sem.a1c, ne[MUP])
            send_c([(MOFF, dst)], "aq", 0, NC, "a1c")
            g.wait_ge(sem.a1p, ne[MUP])
            send_p([(MOFF, dst)], "ap_", 0, NC, "a1p")

    if rank is None:
        if core in P["s_part"]:
            selector(*P["s_part"][core])
        relay_a()
        for r in range(P["n"]):
            if core in P["helpers"][r]:
                lo = slot[r] * NC
                send_v([(MOFF, [cores[q] for q in P["send"][r][core]])], lo, lo + NC, "t%d" % r, ["t%d" % r], ne[MUP])
        if sent[0]:
            g.wait_ge(sem.sent, sent[0])
        return

    me = rank
    group, chip = P["group"], P["chip"]
    cmate = cores[P["partner"][me]]

    if me == root:
        g.sync.dma_start(T.ta[:], T.a[:]).then_inc(sem.ld_a, 16)
    g.sync.dma_start(T.wq[:].bitcast(dt.uint8), T.wc[:]).then_inc(sem.ld_w, 16)
    g.sync.dma_start(T.wp[:], T.ws[:]).then_inc(sem.ld_w, 16)
    g.sync.dma_start(T.tx[:], T.x[:]).then_inc(sem.ld_x, 16)
    g.sync.dma_start(T.tb[:], T.bb[:]).then_inc(sem.ld_b, 16)

    i_s = selector(*P["s_part"][core])
    if me == root:
        g.vector.wait_ge(sem.ld_a, 16)
        i_a = done("dve", g.vector.quantize_mx(T.aq[:], T.ap_[:], T.ta[:]))
    g.vector.wait_ge(sem.ld_x, 16)
    done("dve", g.vector.quantize_mx(T.xq[:], T.xp[:], T.tx[:]))
    g.vector.wait_ge(sem.ld_b, 16)
    i_b = done("dve", g.vector.quantize_mx(T.bq[:], T.bp[:], T.tb[:]))

    a_need = {}
    if me == root:
        g.wait_ge(sem.dve, i_a)
        inside = [c for c in P["a_relay"] if c != cmate] + [cmate]
        ev = [ch for ch in P["gchips"][0] if ch != here]
        send_c([(MUP, inside), (MOFF, [cores[at[(ch, lane[me])]] for ch in ev])], "aq", 0, NC, "a1c")
        send_p([(MUP, inside), (MOFF, [cores[at[(ch, 1 - lane[me])]] for ch in ev])], "ap_", 0, NC, "a1p")
    elif here == chip[root]:
        a_need = {"a1c": ne[MUP], "a1p": ne[MUP]}
        relay_a()
    elif group[me] != group[root]:
        a_need = {"a1c": ne[MOFF], "a1p": ne[MOFF]}
    elif lane[me] == lane[root]:
        a_need = {"a1c": ne[MOFF], "a2": ne[MON]}
        g.wait_ge(sem.a1c, ne[MOFF])
        send_c([(MON, [cmate])], "aq", 0, NC, "a2")
    else:
        a_need = {"a1p": ne[MOFF], "a2": ne[MON]}
        g.wait_ge(sem.a1p, ne[MOFF])
        send_p([(MON, [cmate])], "ap_", 0, NC, "a2")

    def bank(k):
        return T.ps[:, 512 * k:512 * k + NC]

    def tmp(b):
        return T.tmp[:, b * NC:(b + 1) * NC]

    g.tensor.wait_ge(sem.dve, i_s)
    g.tensor.wait_ge(sem.s_in, P["s_calls"][me] * ne[MON])
    g.tensor.wait_ge(sem.ld_w, 32)
    for b in range(4):
        done("pe", g.tensor.matmul_mx(bank(b), T.sq[:, b * NC:(b + 1) * NC], T.sp[:, b * NC:(b + 1) * NC],
                                      T.wq[:], T.wp[:], True, True))
    g.tensor.wait_ge(sem.dve, i_b)
    for q in sorted(a_need):
        g.tensor.wait_ge(sem[q], a_need[q])
    i_m = [done("pe", g.tensor.matmul_mx(bank(4 + b), T.bq[:, b * NC:(b + 1) * NC], T.bp[:, b * NC:(b + 1) * NC],
                                         T.aq[:], T.ap_[:], True, True)) for b in range(4)]
    g.vector.wait_ge(sem.pe, i_m[0])
    i_0 = done("dve", g.vector.tensor_scalar(tmp(0), bank(4), C, None, AluOpType.mult))
    for b in (1, 0, 2, 3):
        if b:
            g.scalar.wait_ge(sem.pe, i_m[b])
            i_c = done("act", g.scalar.activation(tmp(b), bank(4 + b), ActivationFunctionType.Copy, scale=C))
            g.vector.wait_ge(sem.act, i_c)
        else:
            g.vector.wait_ge(sem.dve, i_0)
        i_v = done("dve", g.vector.tensor_tensor(T.tv[:, b:W4:4], bank(b), tmp(b), AluOpType.add))
    s0 = slot[me] * NC
    g.vector.wait_ge(sem.dve, i_v)
    i_q = done("dve", g.vector.quantize_mx(T.vq[:, s0:s0 + NC], T.vp[:, s0:s0 + NC], T.tv[:]))

    g.wait_ge(sem.dve, i_q)
    send_v([(MUP, P["helpers"][me]), (MOFF, [cores[q] for q in P["send"][me][core]])], s0, s0 + NC, "t%d" % me)
    for k in (0, 1):
        lo, hi = P["span"][(lane[me], k)]
        send_v([(MON, [cmate])], lo, hi, "f%d" % k,
               ["t%d" % r for r in P["members"][(lane[me], k)] if r != me], ne[MOFF])
    g.wait_ge(sem.sent, sent[0])

    order = [(me, None)]
    for k in (0, 1):
        order += [(r, "t%d" % r) for r in P["members"][(lane[me], k)] if r != me]
        order += [(r, "f%d" % k) for r in P["members"][(1 - lane[me], k)]]
    copied, where, seen = [], {}, set()
    g.tensor.wait_ge(sem.dve, i_q)
    for i, (r, s) in enumerate(order):
        if s is not None and s not in seen:
            seen.add(s)
            for x in "cp":
                g.tensor.wait_ge(sem[s + x], ne[MOFF] if s[0] == "t" else ne[MON])
        if i >= 8:
            g.tensor.wait_ge(sem[copied[i - 8][0]], copied[i - 8][1])
        lo = slot[r] * NC
        i_y = done("pe", g.tensor.matmul_mx(bank(i % 8), T.vq[:, lo:lo + NC], T.vp[:, lo:lo + NC], T.xq[:], T.xp[:],
                                            True, True))
        dst = T.yo[:, r * NC:(r + 1) * NC]
        if i % 2 == 0:
            g.vector.wait_ge(sem.pe, i_y)
            c = ("dve", done("dve", g.vector.tensor_copy(dst, bank(i % 8))))
        else:
            g.scalar.wait_ge(sem.pe, i_y)
            c = ("act", done("act", g.scalar.activation(dst, bank(i % 8), ActivationFunctionType.Copy)))
        copied.append(c)
        where[r] = c
    nst = 0
    for k in (0, 1):
        for l in (lane[me], 1 - lane[me]):
            runs = []
            for r in sorted(P["members"][(l, k)]):
                if runs and runs[-1][-1] == r - 1:
                    runs[-1].append(r)
                else:
                    runs.append([r])
            for run in runs:
                need = {}
                for r in run:
                    q, v = where[r]
                    need[q] = max(need.get(q, 0), v)
                for q in sorted(need):
                    g.sync.wait_ge(sem[q], need[q])
                c0, c1 = run[0] * NC, (run[-1] + 1) * NC
                g.sync.dma_start(T.y[:, c0:c1], T.yo[:, c0:c1]).then_inc(sem.st, 16)
                nst += 16
    g.sync.wait_ge(sem.st, nst)
